import numpy as np
import ml_dtypes


def mxq(x, axis, fmt="e4m3"):
    dtype, down = {"e4m3": (ml_dtypes.float8_e4m3fn, 7), "e5m2": (ml_dtypes.float8_e5m2, 14)}[fmt]
    v = np.moveaxis(np.asarray(x, np.float32).astype(ml_dtypes.bfloat16).astype(np.float64), axis, -1)
    blocks = v.reshape(v.shape[:-1] + (-1, 32))
    amax = np.abs(blocks).max(-1, keepdims=True)
    byte = np.maximum(np.where(amax > 0, np.frexp(amax)[1] - 1 + 127, 0) - down, 1)
    scale = np.exp2(byte - 127.0)
    codes = (blocks / scale).astype(np.float32).astype(dtype).astype(np.float64)
    return np.moveaxis((codes * scale).reshape(v.shape), -1, axis)


WIDE = False


def mx_kscale(k):
    if not WIDE:
        return np.ones(k)
    levels = np.array([10, -10, 5, -5, 0])
    if k % 512:
        return np.exp2(np.random.permutation(np.resize(levels, k // 32))).repeat(32)
    a = np.empty((k // 512, 16))
    for p in range(k // 512):
        a[p, :8] = np.random.permutation(np.resize(levels, 8))
        for g in range(8):
            far = levels[np.abs(levels - a[p, g]) >= 10]
            a[p, g + 8] = far[np.random.randint(len(far))]
    return np.exp2(a.ravel()).repeat(32)


def f64(x):
    return np.asarray(x).astype(np.float64)


def striped(idx):
    return np.tile(idx.reshape(-1, 16).T, (8, 1)).astype(np.uint16)


def unstriped(offs):
    return offs[:16].T.reshape(-1).astype(np.int64)


E2M1 = np.array([0.0, 0.5, 1.0, 1.5, 2.0, 3.0, 4.0, 6.0, -0.0, -0.5, -1.0, -1.5, -2.0, -3.0, -4.0, -6.0])


def pack_weight(w, fmt):
    k, n = w.shape
    w = f64(np.asarray(w, np.float32).astype(ml_dtypes.bfloat16)).reshape(k // 32, 32, n)
    amax = np.abs(w).max(1)
    if fmt == "e4m3":
        byte = np.frexp(amax)[1] - 1 + 127 - 7
    else:
        mant, ex = np.frexp(amax / 6.0)
        byte = np.where(mant > 0.5, ex, ex - 1) + 127
    byte = np.clip(np.where(amax > 0, byte, 1), 1, 254)
    scaled = (w * np.exp2(127.0 - byte)[:, None, :]).reshape(k, n).astype(np.float32)
    by_word = np.ascontiguousarray(scaled.reshape(k // 512, 128, 4, n).transpose(0, 1, 3, 2))
    if fmt == "e4m3":
        words = by_word.astype(ml_dtypes.float8_e4m3fn).view(np.uint8)
    else:
        c = by_word.astype(ml_dtypes.float4_e2m1fn).view(np.uint8) & 0xF
        words = (c[..., 0::2] | (c[..., 1::2] << 4)).reshape(k // 512, 128, 2 * n)
    return np.ascontiguousarray(words), np.ascontiguousarray(byte.astype(np.uint8).reshape(k // 512, 16, n))


def unpack_weight(words, scales, fmt):
    g, _, n = scales.shape
    words = np.ascontiguousarray(words).reshape(g, 128, n, -1)
    if fmt == "e4m3":
        vals = words.view(ml_dtypes.float8_e4m3fn).astype(np.float64)
    else:
        nib = np.empty((g, 128, n, 4), np.uint8)
        nib[..., 0::2] = words & 0xF
        nib[..., 1::2] = words >> 4
        vals = E2M1[nib]
    vals = vals * np.repeat(np.exp2(scales.astype(np.float64) - 127.0), 8, axis=1)[..., None]
    return vals.transpose(0, 1, 3, 2).reshape(g * 512, n)


def gelu(v):
    return 0.5 * v * (1.0 + np.tanh(np.sqrt(2.0 / np.pi) * (v + 0.044715 * v**3)))


def twice(P):
    return np.random.permutation(np.repeat(np.arange(P), 2))


K, H, T, S, P = 512, 1024, 4096, 1024, 512


def setup_inputs():
    n = np.random.standard_normal
    s = mx_kscale(K)[:, None]
    u = mx_kscale(H)[:, None]
    d = {}
    d["tab_words"], d["tab_scales"] = pack_weight(n((K, T)) * s, "e4m3")
    d["offs"] = striped(np.random.permutation(T)[:S])
    d["w1"] = (n((K, H)) / s / K ** 0.5).astype(np.float32)
    d["w4_words"], d["w4_scales"] = pack_weight(n((K, H)) / s / K ** 0.5, "e2m1")
    d["gu"] = (np.exp(0.3 * n(H)) * u[:, 0]).astype(np.float32)
    d["pos1"] = striped(np.random.permutation(S)[:P])
    d["pos2"] = striped(np.random.permutation(S)[:P])
    d["w2"] = (0.42 * n((H, H)) / u / H ** 0.5).astype(np.float32)
    d["w8_words"], d["w8_scales"] = pack_weight(0.42 * n((H, H)) / u / H ** 0.5, "e4m3")
    d["pos3"] = striped(twice(P))
    d["gs"] = (0.7 * np.exp(0.3 * n(H)) / u[:, 0]).astype(np.float32)
    return d


def reference(tab_words, tab_scales, offs, w1, w4_words, w4_scales, gu, pos1, pos2,
              w2, w8_words, w8_scales, pos3, gs):
    v = unpack_weight(tab_words, tab_scales, "e4m3")[:, unstriped(offs)]
    w4 = unpack_weight(w4_words, w4_scales, "e2m1")
    w8 = unpack_weight(w8_words, w8_scales, "e4m3")
    diff = w4.T @ v - mxq(f64(w1), 0, "e4m3").T @ v
    h = diff / (1.0 + np.exp(-diff)) * f64(gu)[:, None]
    x = np.maximum(h[:, unstriped(pos1)], h[:, unstriped(pos2)])
    xq = mxq(x, 0, "e4m3")
    y = np.maximum(mxq(f64(w2), 0, "e4m3").T @ xq, w8.T @ xq)
    return np.cos(y[:, unstriped(pos3)]) + f64(gs)[:, None] * h

@@ -1,0 +1,286 @@
+import math
+from contextlib import ExitStack
+
+import concourse.mybir as mybir
+
+K, H, T, S, NP = 512, 1024, 4096, 1024, 512
+FLOPS = 2 * (2 * K * H * S) + 2 * (2 * H * H * NP)
+
+F32 = mybir.dt.float32
+BF16 = mybir.dt.bfloat16
+I32 = mybir.dt.int32
+U32 = mybir.dt.uint32
+U16 = mybir.dt.uint16
+U8 = mybir.dt.uint8
+FP8X4 = mybir.dt.float8_e4m3fn_x4
+FP4X4 = mybir.dt.float4_e2m1fn_x4
+ALU = mybir.AluOpType
+ACT = mybir.ActivationFunctionType
+
+P = 128
+N = 512
+SLICES = H // P
+TURN_OFFSET = float(2 ** 21)
+
+
+def tile_list_brush_pressure_advice_kernel(
+    tc, tab_words, tab_scales, offs, w1, w4_words, w4_scales, gu, pos1, pos2, w2, w8_words, w8_scales, pos3, gs, out
+):
+    nc = tc.nc
+    with ExitStack() as ctx:
+        lists = ctx.enter_context(tc.tile_pool(name="lists", bufs=1))
+        keep = ctx.enter_context(tc.tile_pool(name="keep", bufs=1))
+        ring = ctx.enter_context(tc.tile_pool(name="ring", bufs=1))
+        psum = ctx.enter_context(tc.psum_pool(name="psum", bufs=8))
+
+        def held(shape, dtype, name):
+            return keep.tile(shape, dtype, name=name, align_bytes=64)
+
+        def staged(shape, dtype, name, tag, bufs=1):
+            return ring.tile(shape, dtype, name=name, tag=tag, bufs=bufs, align_bytes=64)
+
+        warm = staged([P, 2], F32, "warm", "slot3")
+        tab_s = staged([P, T], U8, "tab_s", "slot2")
+        w4_s_raw = staged([P, H], U8, "w4_s_raw", "planes")
+        nc.vector.memset(warm[:, 0:1], 0.0)
+        nc.vector.memset(tab_s[:].bitcast(I32), 0)
+        nc.vector.memset(w4_s_raw[:].bitcast(I32), 0)
+        nc.scalar.activation(warm[:, 1:2], warm[:, 0:1], ACT.Silu)
+
+        offs_t = lists.tile([P, S // 16], U16, name="offs_t")
+        pos1_t = lists.tile([P, NP // 16], U16, name="pos1_t")
+        pos2_t = lists.tile([P, NP // 16], U16, name="pos2_t")
+        pos3_t = lists.tile([P, S // 16], U16, name="pos3_t")
+        for tile, src in ((offs_t, offs), (pos1_t, pos1), (pos2_t, pos2), (pos3_t, pos3)):
+            nc.sync.dma_start(tile[:], src)
+
+        gu_t = held([P, 2, 4], F32, "gu_t")
+        gs_t = held([P, 2, 4], F32, "gs_t")
+        nc.gpsimd.dma_start(gu_t[:], gu.rearrange("(b p t) -> p b t", b=2, t=4))
+        nc.gpsimd.dma_start(gs_t[:], gs.rearrange("(b p t) -> p b t", b=2, t=4))
+
+        def load_rows(w, a, cols, name, tag):
+            raw = staged([P, 4, cols.stop - cols.start], F32, name, tag)
+            nc.sync.dma_start(raw[:], w[N * a : N * (a + 1), cols].rearrange("(p j) c -> p j c", j=4))
+            return raw
+
+        w4_raw = staged([P, 2 * H], U8, "w4_raw", "slot1")
+        nc.sync.dma_start(w4_raw[:].bitcast(I32), w4_words[0].bitcast(I32))
+        w1_raw0 = load_rows(w1, 0, slice(0, N), "w1_raw0", "slot0")
+        for q in range(4):
+            nc.sync.dma_start(
+                tab_s[32 * q : 32 * q + 4, :].bitcast(I32), tab_scales[0, 4 * q : 4 * q + 4, :].bitcast(I32)
+            )
+        tab_w = staged([P, T], U32, "tab_w", "slot3")
+        nc.sync.dma_start(tab_w[:].bitcast(I32), tab_words[0].rearrange("p t i -> p (t i)").bitcast(I32))
+        for q in range(4):
+            nc.scalar.dma_start(
+                w4_s_raw[32 * q : 32 * q + 4, :].bitcast(I32), w4_scales[0, 4 * q : 4 * q + 4, :].bitcast(I32)
+            )
+
+        def cast_views(raw_cols, name):
+            grouped = staged([P, 4 * N], BF16, name, "grouped", bufs=3)
+            dst = grouped[:].rearrange("p (t m j) -> p m t j", t=4, j=4)
+            src = raw_cols.rearrange("p j (m t) -> p m t j", t=4)
+            return grouped, dst, src
+
+        def quantize(grouped, name):
+            codes = held([P, N], U32, name + "_c")
+            scales = held([P, N], U8, name + "_s")
+            nc.vector.quantize_mx(out=codes[:].bitcast(FP8X4), scales=scales[:], in_=grouped[:])
+            return codes, scales
+
+        w4_c = held([P, 2 * H], U8, "w4_c")
+        w4_s = held([P, H], U8, "w4_s")
+        for b in range(2):
+            cols = slice(H * b, H * (b + 1))
+            nc.vector.tensor_copy(
+                w4_c[:, cols].rearrange("p (t c i e) -> p c t i e", t=4, i=8, e=2),
+                w4_raw[:, cols].rearrange("p (c i t e) -> p c t i e", t=4, i=8, e=2),
+            )
+
+        grouped, dst, src = cast_views(w1_raw0[:], "w1_g0")
+        nc.vector.tensor_scalar(dst, src, -1.0, None, op0=ALU.mult)
+        w1_q = [quantize(grouped, "w1_0")]
+
+        gains = held([P, SLICES, N], F32, "gains")
+        gu_cols = gu_t[:].rearrange("p b t -> p (b t)")
+        for s in range(SLICES):
+            nc.scalar.activation(gains[:, s, :], gu_cols[:, s : s + 1].to_broadcast([P, N]), ACT.Copy)
+
+        v_s = held([P, S], U8, "v_s")
+        nc.vector.tensor_copy(v_s[:], tab_s[:].indirect(offs_t[:]))
+        nc.vector.tensor_copy(
+            w4_s[:].rearrange("p (b t c i) -> p b c t i", b=2, t=4, i=16),
+            w4_s_raw[:].rearrange("p (b c i t) -> p b c t i", b=2, t=4, i=16),
+        )
+        v_w = []
+        for u in range(2):
+            words = held([P, N], U32, f"v_w{u}")
+            nc.vector.tensor_copy(words[:], tab_w[:].indirect(offs_t[:, 32 * u : 32 * (u + 1)]))
+            v_w.append(words)
+
+        w1_raw1 = load_rows(w1, 0, slice(N, H), "w1_raw1", "slot1")
+        w8_raw = staged([P, 2, H], I32, "w8_raw", "slot2")
+        nc.sync.dma_start(w8_raw[:], w8_words.rearrange("a p c i -> p a (c i)").bitcast(I32))
+        w8_s_raw = staged([P, H], U8, "w8_s_raw", "planes")
+        nc.vector.memset(w8_s_raw[:].bitcast(I32), 0)
+        for q in range(4):
+            nc.sync.dma_start(
+                w8_s_raw[32 * q : 32 * q + 8, :].bitcast(I32), w8_scales[:, 4 * q : 4 * q + 4, :].bitcast(I32)
+            )
+        w2_raw = {}
+        w2_raw[1, 0] = load_rows(w2, 1, slice(0, N), "w2_raw10", "slot0")[:]
+        w2_raw0 = load_rows(w2, 0, slice(0, H), "w2_raw0", "slot3")
+        w2_raw[0, 0] = w2_raw0[:, :, 0:N]
+        w2_raw[0, 1] = w2_raw0[:, :, N:H]
+
+        gg = held([P, SLICES], F32, "gg")
+        nc.vector.tensor_tensor(gg[:], gu_cols, gs_t[:].rearrange("p b t -> p (b t)"), ALU.mult)
+
+        def cast_on_scalar(raw_cols, name, scale):
+            grouped, dst, src = cast_views(raw_cols, name)
+            nc.scalar.activation(dst, src, ACT.Copy, scale=scale)
+            return grouped
+
+        silu = [held([P, S], F32, f"silu{s}") for s in range(SLICES)]
+
+        def stage1(s):
+            b, t = divmod(s, 4)
+            w1_c, w1_s = w1_q[b]
+            for u in range(2):
+                cols = slice(N * u, N * (u + 1))
+                acc = psum.tile([P, N], F32, name="acc", tag="bank")
+                nc.tensor.matmul_mx(
+                    out=acc[:],
+                    lhsT=w4_c[:, 2 * P * s : 2 * P * (s + 1)].bitcast(FP4X4),
+                    lhsT_scale=w4_s[:, P * s : P * (s + 1)],
+                    rhs=v_w[u][:].bitcast(FP8X4),
+                    rhs_scale=v_s[:, cols],
+                    start=True,
+                    stop=False,
+                )
+                nc.tensor.matmul_mx(
+                    out=acc[:],
+                    lhsT=w1_c[:, P * t : P * (t + 1)].bitcast(FP8X4),
+                    lhsT_scale=w1_s[:, P * t : P * (t + 1)],
+                    rhs=v_w[u][:].bitcast(FP8X4),
+                    rhs_scale=v_s[:, cols],
+                    start=False,
+                    stop=True,
+                )
+                nc.scalar.activation(silu[s][:, cols], acc[:], ACT.Silu)
+
+        def pick(s, first, second):
+            t = s % 4
+            nc.vector.tensor_tensor(first[:, t, :], silu[s][:].indirect(pos1_t[:]), gains[:, s, :], ALU.mult)
+            nc.vector.tensor_tensor(second[:, t, :], silu[s][:].indirect(pos2_t[:]), gains[:, s, :], ALU.mult)
+            nc.scalar.activation(silu[s][:], silu[s][:], ACT.Copy, scale=gg[:, s : s + 1], bias=-1.0)
+
+        def larger(first, second, b):
+            grouped = staged([P, 4 * N], BF16, f"x_g{b}", "grouped", bufs=3)
+            nc.vector.tensor_tensor(
+                grouped[:].rearrange("p (c i t) -> p c t i", i=4, t=4),
+                first[:].rearrange("p t (c i) -> p c t i", i=4),
+                second[:].rearrange("p t (c i) -> p c t i", i=4),
+                ALU.max,
+            )
+            return quantize(grouped, f"x_{b}")
+
+        x_q = []
+        w2_q = {}
+        for s in range(4):
+            stage1(s)
+        w1_q.append(quantize(cast_on_scalar(w1_raw1[:], "w1_g1", -1.0), "w1_1"))
+        w2_raw[1, 1] = load_rows(w2, 1, slice(N, H), "w2_raw11", "slot1")[:]
+        for s in range(4, SLICES):
+            stage1(s)
+
+        w8_c = held([P, 2, H], I32, "w8_c")
+        w8_s = held([P, H], U8, "w8_s")
+        for b in range(2):
+            first = staged([P, 4, N], F32, f"first{b}", "picked", bufs=4)
+            second = staged([P, 4, N], F32, f"second{b}", "picked", bufs=4)
+            for t in range(4):
+                pick(4 * b + t, first, second)
+            x_q.append(larger(first, second, b))
+            if b == 0:
+                for a in range(2):
+                    nc.vector.tensor_copy(
+                        w8_c[:, a, :].rearrange("p (b t c i) -> p b c t i", b=2, t=4, i=4),
+                        w8_raw[:, a, :].rearrange("p (b c i t) -> p b c t i", b=2, t=4, i=4),
+                    )
+                nc.vector.tensor_copy(
+                    w8_s[:].rearrange("p (b t c i) -> p b c t i", b=2, t=4, i=16),
+                    w8_s_raw[:].rearrange("p (b c i t) -> p b c t i", b=2, t=4, i=16),
+                )
+                for c in range(2):
+                    for a in (1, 0):
+                        w2_q[a, c] = quantize(cast_on_scalar(w2_raw[a, c], f"w2_g{a}{c}", 1.0), f"w2_{a}{c}")
+
+        out_rows = out.rearrange("(b p t) j -> b t p j", b=2, t=4)
+        work = {}
+
+        def products(s):
+            b, t = divmod(s, 4)
+            m_cols = slice(P * t, P * (t + 1))
+            n_cols = slice(P * s, P * (s + 1))
+            acc2 = psum.tile([P, N], F32, name="acc2", tag="bank")
+            acc8 = psum.tile([P, N], F32, name="acc8", tag="bank")
+            for a in range(2):
+                nc.tensor.matmul_mx(
+                    out=acc8[:],
+                    lhsT=w8_c[:, a, n_cols].bitcast(FP8X4),
+                    lhsT_scale=w8_s[4 * a :, n_cols],
+                    rhs=x_q[a][0][:].bitcast(FP8X4),
+                    rhs_scale=x_q[a][1][:],
+                    start=(a == 0),
+                    stop=(a == 1),
+                )
+            for a in range(2):
+                nc.tensor.matmul_mx(
+                    out=acc2[:],
+                    lhsT=w2_q[a, b][0][:, m_cols].bitcast(FP8X4),
+                    lhsT_scale=w2_q[a, b][1][:, m_cols],
+                    rhs=x_q[a][0][:].bitcast(FP8X4),
+                    rhs_scale=x_q[a][1][:],
+                    start=(a == 0),
+                    stop=(a == 1),
+                )
+            work[s] = staged([P, 3 * N], F32, f"work{s}", "work", bufs=4)
+            w_b, w_c = work[s][:, N : 2 * N], work[s][:, 2 * N : 3 * N]
+            nc.scalar.activation(w_b, acc8[:], ACT.Copy, scale=1.0 / (2.0 * math.pi))
+            nc.vector.scalar_tensor_tensor(w_c, acc2[:], 1.0 / (2.0 * math.pi), w_b, ALU.mult, ALU.max)
+
+        def reduce_turns(s):
+            w_a, w_c = work[s][:, 0:N], work[s][:, 2 * N : 3 * N]
+            whole = staged([P, N], U32, f"whole{s}", "whole", bufs=3)
+            nc.scalar.activation(whole[:], w_c, ACT.Copy, bias=TURN_OFFSET + 0.75)
+            nc.vector.scalar_tensor_tensor(
+                w_a, whole[:].bitcast(I32), TURN_OFFSET + 0.5, w_c, ALU.subtract, ALU.subtract
+            )
+
+        def finish(s):
+            b, t = divmod(s, 4)
+            w_a, w_b = work[s][:, 0:N], work[s][:, N : 2 * N]
+            nc.scalar.activation(w_b, w_a, ACT.Sin, scale=math.pi)
+            nc.scalar.activation(w_a, w_b, ACT.Square, scale=math.sqrt(2.0))
+            result = staged([P, S], F32, f"result{s}", "picked", bufs=4)
+            if s < SLICES - 1:
+                nc.vector.tensor_tensor(result[:], work[s][:].indirect(pos3_t[:]), silu[s][:], ALU.add)
+                nc.sync.dma_start(out_rows[b, t], result[:])
+            else:
+                for u in range(2):
+                    cols = slice(N * u, N * (u + 1))
+                    nc.vector.tensor_tensor(
+                        result[:, cols], work[s][:].indirect(pos3_t[:, 32 * u : 32 * (u + 1)]), silu[s][:, cols], ALU.add
+                    )
+                    nc.sync.dma_start(out_rows[b, t][:, cols], result[:, cols])
+
+        for step in range(SLICES + 2):
+            if step < SLICES:
+                products(step)
+            if 1 <= step <= SLICES:
+                reduce_turns(step - 1)
+            if step >= 2:
+                finish(step - 2)

@@ -39,13 +39,14 @@ def tile_list_brush_pressure_advice_kernel(
         def staged(shape, dtype, name, tag, bufs=1):
             return ring.tile(shape, dtype, name=name, tag=tag, bufs=bufs, align_bytes=64)
 
-        warm = staged([P, 2], F32, "warm", "slot3")
+        warm_in = staged([P, 1], F32, "warm_in", "slot3")
+        warm_out = staged([P, 1], F32, "warm_out", "planes")
         tab_s = staged([P, T], U8, "tab_s", "slot2")
-        w4_s_raw = staged([P, H], U8, "w4_s_raw", "planes")
-        nc.vector.memset(warm[:, 0:1], 0.0)
         nc.vector.memset(tab_s[:].bitcast(I32), 0)
+        nc.vector.memset(warm_in[:], 0.0)
+        nc.scalar.activation(warm_out[:], warm_in[:], ACT.Silu)
+        w4_s_raw = staged([P, H], U8, "w4_s_raw", "planes")
         nc.vector.memset(w4_s_raw[:].bitcast(I32), 0)
-        nc.scalar.activation(warm[:, 1:2], warm[:, 0:1], ACT.Silu)
 
         offs_t = lists.tile([P, S // 16], U16, name="offs_t")
         pos1_t = lists.tile([P, NP // 16], U16, name="pos1_t")
@@ -57,35 +58,36 @@ def tile_list_brush_pressure_advice_kernel(
         gu_t = held([P, 2, 4], F32, "gu_t")
         gs_t = held([P, 2, 4], F32, "gs_t")
         nc.gpsimd.dma_start(gu_t[:], gu.rearrange("(b p t) -> p b t", b=2, t=4))
-        nc.gpsimd.dma_start(gs_t[:], gs.rearrange("(b p t) -> p b t", b=2, t=4))
 
         def load_rows(w, a, cols, name, tag):
             raw = staged([P, 4, cols.stop - cols.start], F32, name, tag)
             nc.sync.dma_start(raw[:], w[N * a : N * (a + 1), cols].rearrange("(p j) c -> p j c", j=4))
             return raw
 
-        w4_raw = staged([P, 2 * H], U8, "w4_raw", "slot1")
+        w4_raw = held([P, 2 * H], U8, "w4_raw")
         nc.sync.dma_start(w4_raw[:].bitcast(I32), w4_words[0].bitcast(I32))
+
+        def load_scale_rows(queue, plane, scales, quadrants):
+            for q in quadrants:
+                queue.dma_start(
+                    plane[32 * q : 32 * q + 4, :].bitcast(I32), scales[0, 4 * q : 4 * q + 4, :].bitcast(I32)
+                )
+
         w1_raw0 = load_rows(w1, 0, slice(0, N), "w1_raw0", "slot0")
-        for q in range(4):
-            nc.sync.dma_start(
-                tab_s[32 * q : 32 * q + 4, :].bitcast(I32), tab_scales[0, 4 * q : 4 * q + 4, :].bitcast(I32)
-            )
+        load_scale_rows(nc.sync, tab_s, tab_scales, range(4))
+        nc.gpsimd.dma_start(gs_t[:], gs.rearrange("(b p t) -> p b t", b=2, t=4))
         tab_w = staged([P, T], U32, "tab_w", "slot3")
         nc.sync.dma_start(tab_w[:].bitcast(I32), tab_words[0].rearrange("p t i -> p (t i)").bitcast(I32))
-        for q in range(4):
-            nc.scalar.dma_start(
-                w4_s_raw[32 * q : 32 * q + 4, :].bitcast(I32), w4_scales[0, 4 * q : 4 * q + 4, :].bitcast(I32)
-            )
+        load_scale_rows(nc.sync, w4_s_raw, w4_scales, range(4))
 
-        def cast_views(raw_cols, name):
-            grouped = staged([P, 4 * N], BF16, name, "grouped", bufs=3)
+        def cast_views(raw_cols, name, tag="grouped", bufs=3):
+            grouped = staged([P, 4 * N], BF16, name, tag, bufs=bufs)
             dst = grouped[:].rearrange("p (t m j) -> p m t j", t=4, j=4)
             src = raw_cols.rearrange("p j (m t) -> p m t j", t=4)
             return grouped, dst, src
 
         def quantize(grouped, name):
-            codes = held([P, N], U32, name + "_c")
+            codes = staged([P, N], U32, name + "_c", name + "_c")
             scales = held([P, N], U8, name + "_s")
             nc.vector.quantize_mx(out=codes[:].bitcast(FP8X4), scales=scales[:], in_=grouped[:])
             return codes, scales
@@ -99,9 +101,11 @@ def tile_list_brush_pressure_advice_kernel(
                 w4_raw[:, cols].rearrange("p (c i t e) -> p c t i e", t=4, i=8, e=2),
             )
 
-        grouped, dst, src = cast_views(w1_raw0[:], "w1_g0")
+        grouped, dst, src = cast_views(w1_raw0[:], "w1_g0", "slot1", 1)
         nc.vector.tensor_scalar(dst, src, -1.0, None, op0=ALU.mult)
         w1_q = [quantize(grouped, "w1_0")]
+        w8_raw = staged([P, 2, H], I32, "w8_raw", "slot0")
+        nc.sync.dma_start(w8_raw[:], w8_words.rearrange("a p c i -> p a (c i)").bitcast(I32))
 
         gains = held([P, SLICES, N], F32, "gains")
         gu_cols = gu_t[:].rearrange("p b t -> p (b t)")
@@ -114,29 +118,24 @@ def tile_list_brush_pressure_advice_kernel(
             w4_s[:].rearrange("p (b t c i) -> p b c t i", b=2, t=4, i=16),
             w4_s_raw[:].rearrange("p (b c i t) -> p b c t i", b=2, t=4, i=16),
         )
-        v_w = []
+        v_w = [staged([P, N], U32, "v_w0", "slot2")[:], staged([P, N], U32, "v_w1", "planes")[:]]
         for u in range(2):
-            words = held([P, N], U32, f"v_w{u}")
-            nc.vector.tensor_copy(words[:], tab_w[:].indirect(offs_t[:, 32 * u : 32 * (u + 1)]))
-            v_w.append(words)
+            nc.vector.tensor_copy(v_w[u], tab_w[:].indirect(offs_t[:, 32 * u : 32 * (u + 1)]))
+        w8_c = held([P, 2, H], I32, "w8_c")
+        for a in range(2):
+            nc.vector.tensor_copy(
+                w8_c[:, a, :].rearrange("p (b t c i) -> p b c t i", b=2, t=4, i=4),
+                w8_raw[:, a, :].rearrange("p (b c i t) -> p b c t i", b=2, t=4, i=4),
+            )
 
         w1_raw1 = load_rows(w1, 0, slice(N, H), "w1_raw1", "slot1")
-        w8_raw = staged([P, 2, H], I32, "w8_raw", "slot2")
-        nc.sync.dma_start(w8_raw[:], w8_words.rearrange("a p c i -> p a (c i)").bitcast(I32))
-        w8_s_raw = staged([P, H], U8, "w8_s_raw", "planes")
-        nc.vector.memset(w8_s_raw[:].bitcast(I32), 0)
-        for q in range(4):
-            nc.sync.dma_start(
-                w8_s_raw[32 * q : 32 * q + 8, :].bitcast(I32), w8_scales[:, 4 * q : 4 * q + 4, :].bitcast(I32)
-            )
         w2_raw = {}
-        w2_raw[1, 0] = load_rows(w2, 1, slice(0, N), "w2_raw10", "slot0")[:]
         w2_raw0 = load_rows(w2, 0, slice(0, H), "w2_raw0", "slot3")
         w2_raw[0, 0] = w2_raw0[:, :, 0:N]
         w2_raw[0, 1] = w2_raw0[:, :, N:H]
 
         gg = held([P, SLICES], F32, "gg")
-        nc.vector.tensor_tensor(gg[:], gu_cols, gs_t[:].rearrange("p b t -> p (b t)"), ALU.mult)
+        nc.gpsimd.tensor_tensor(gg[:], gu_cols, gs_t[:].rearrange("p b t -> p (b t)"), ALU.mult)
 
         def cast_on_scalar(raw_cols, name, scale):
             grouped, dst, src = cast_views(raw_cols, name)
@@ -155,7 +154,7 @@ def tile_list_brush_pressure_advice_kernel(
                     out=acc[:],
                     lhsT=w4_c[:, 2 * P * s : 2 * P * (s + 1)].bitcast(FP4X4),
                     lhsT_scale=w4_s[:, P * s : P * (s + 1)],
-                    rhs=v_w[u][:].bitcast(FP8X4),
+                    rhs=v_w[u].bitcast(FP8X4),
                     rhs_scale=v_s[:, cols],
                     start=True,
                     stop=False,
@@ -164,7 +163,7 @@ def tile_list_brush_pressure_advice_kernel(
                     out=acc[:],
                     lhsT=w1_c[:, P * t : P * (t + 1)].bitcast(FP8X4),
                     lhsT_scale=w1_s[:, P * t : P * (t + 1)],
-                    rhs=v_w[u][:].bitcast(FP8X4),
+                    rhs=v_w[u].bitcast(FP8X4),
                     rhs_scale=v_s[:, cols],
                     start=False,
                     stop=True,
@@ -175,6 +174,8 @@ def tile_list_brush_pressure_advice_kernel(
             t = s % 4
             nc.vector.tensor_tensor(first[:, t, :], silu[s][:].indirect(pos1_t[:]), gains[:, s, :], ALU.mult)
             nc.vector.tensor_tensor(second[:, t, :], silu[s][:].indirect(pos2_t[:]), gains[:, s, :], ALU.mult)
+
+        def own_part(s):
             nc.scalar.activation(silu[s][:], silu[s][:], ACT.Copy, scale=gg[:, s : s + 1], bias=-1.0)
 
         def larger(first, second, b):
@@ -191,32 +192,38 @@ def tile_list_brush_pressure_advice_kernel(
         w2_q = {}
         for s in range(4):
             stage1(s)
+        w8_s_raw = staged([P, H], U8, "w8_s_raw", "w1_0_c")
+        nc.vector.memset(w8_s_raw[:].bitcast(I32), 0)
+        for q in range(4):
+            nc.sync.dma_start(
+                w8_s_raw[32 * q : 32 * q + 8, :].bitcast(I32), w8_scales[:, 4 * q : 4 * q + 4, :].bitcast(I32)
+            )
         w1_q.append(quantize(cast_on_scalar(w1_raw1[:], "w1_g1", -1.0), "w1_1"))
-        w2_raw[1, 1] = load_rows(w2, 1, slice(N, H), "w2_raw11", "slot1")[:]
+        w2_raw[1, 0] = load_rows(w2, 1, slice(0, N), "w2_raw10", "slot1")[:]
         for s in range(4, SLICES):
             stage1(s)
 
-        w8_c = held([P, 2, H], I32, "w8_c")
         w8_s = held([P, H], U8, "w8_s")
         for b in range(2):
-            first = staged([P, 4, N], F32, f"first{b}", "picked", bufs=4)
-            second = staged([P, 4, N], F32, f"second{b}", "picked", bufs=4)
+            if b == 0:
+                first = staged([P, 4, N], F32, f"first{b}", "slot0")
+            else:
+                first = staged([P, 4, N], F32, f"first{b}", "picked", bufs=3)
+            second = staged([P, 4, N], F32, f"second{b}", "picked", bufs=3)
             for t in range(4):
                 pick(4 * b + t, first, second)
             x_q.append(larger(first, second, b))
             if b == 0:
-                for a in range(2):
-                    nc.vector.tensor_copy(
-                        w8_c[:, a, :].rearrange("p (b t c i) -> p b c t i", b=2, t=4, i=4),
-                        w8_raw[:, a, :].rearrange("p (b c i t) -> p b c t i", b=2, t=4, i=4),
-                    )
+                w2_raw[1, 1] = load_rows(w2, 1, slice(N, H), "w2_raw11", "slot0")[:]
                 nc.vector.tensor_copy(
                     w8_s[:].rearrange("p (b t c i) -> p b c t i", b=2, t=4, i=16),
                     w8_s_raw[:].rearrange("p (b c i t) -> p b c t i", b=2, t=4, i=16),
                 )
                 for c in range(2):
-                    for a in (1, 0):
+                    for a in range(2):
                         w2_q[a, c] = quantize(cast_on_scalar(w2_raw[a, c], f"w2_g{a}{c}", 1.0), f"w2_{a}{c}")
+                for s in range(4):
+                    own_part(s)
 
         out_rows = out.rearrange("(b p t) j -> b t p j", b=2, t=4)
         work = {}
@@ -265,15 +272,15 @@ def tile_list_brush_pressure_advice_kernel(
             w_a, w_b = work[s][:, 0:N], work[s][:, N : 2 * N]
             nc.scalar.activation(w_b, w_a, ACT.Sin, scale=math.pi)
             nc.scalar.activation(w_a, w_b, ACT.Square, scale=math.sqrt(2.0))
-            result = staged([P, S], F32, f"result{s}", "picked", bufs=4)
+            result = staged([P, S], F32, f"result{s}", "picked", bufs=3)
             if s < SLICES - 1:
                 nc.vector.tensor_tensor(result[:], work[s][:].indirect(pos3_t[:]), silu[s][:], ALU.add)
                 nc.sync.dma_start(out_rows[b, t], result[:])
             else:
-                for u in range(2):
-                    cols = slice(N * u, N * (u + 1))
+                for lo, hi in ((0, 512), (512, 768), (768, 1024)):
+                    cols = slice(lo, hi)
                     nc.vector.tensor_tensor(
-                        result[:, cols], work[s][:].indirect(pos3_t[:, 32 * u : 32 * (u + 1)]), silu[s][:, cols], ALU.add
+                        result[:, cols], work[s][:].indirect(pos3_t[:, lo // 16 : hi // 16]), silu[s][:, cols], ALU.add
                     )
                     nc.sync.dma_start(out_rows[b, t][:, cols], result[:, cols])
 
@@ -284,3 +291,5 @@ def tile_list_brush_pressure_advice_kernel(
                 reduce_turns(step - 1)
             if step >= 2:
                 finish(step - 2)
+                if step + 2 < SLICES:
+                    own_part(step + 2)

@@ -40,13 +40,15 @@ def tile_list_brush_pressure_advice_kernel(
             return ring.tile(shape, dtype, name=name, tag=tag, bufs=bufs, align_bytes=64)
 
         warm_in = staged([P, 1], F32, "warm_in", "slot3")
-        warm_out = staged([P, 1], F32, "warm_out", "planes")
+        warm_out = held([P, 1], F32, "warm_out")
         tab_s = staged([P, T], U8, "tab_s", "slot2")
         nc.vector.memset(tab_s[:].bitcast(I32), 0)
+        w4_s_raw = held([P, H], U8, "w4_s_raw")
+        nc.vector.memset(w4_s_raw[:].bitcast(I32), 0)
         nc.vector.memset(warm_in[:], 0.0)
         nc.scalar.activation(warm_out[:], warm_in[:], ACT.Silu)
-        w4_s_raw = staged([P, H], U8, "w4_s_raw", "planes")
-        nc.vector.memset(w4_s_raw[:].bitcast(I32), 0)
+        v_s = held([P, S], U8, "v_s")
+        nc.vector.memset(v_s[:].bitcast(I32), 0)
 
         offs_t = lists.tile([P, S // 16], U16, name="offs_t")
         pos1_t = lists.tile([P, NP // 16], U16, name="pos1_t")
@@ -67,18 +69,13 @@ def tile_list_brush_pressure_advice_kernel(
         w4_raw = held([P, 2 * H], U8, "w4_raw")
         nc.sync.dma_start(w4_raw[:].bitcast(I32), w4_words[0].bitcast(I32))
 
-        def load_scale_rows(queue, plane, scales, quadrants):
-            for q in quadrants:
-                queue.dma_start(
-                    plane[32 * q : 32 * q + 4, :].bitcast(I32), scales[0, 4 * q : 4 * q + 4, :].bitcast(I32)
-                )
-
         w1_raw0 = load_rows(w1, 0, slice(0, N), "w1_raw0", "slot0")
-        load_scale_rows(nc.sync, tab_s, tab_scales, range(4))
+        nc.sync.dma_start(tab_s[0:16, :].bitcast(I32), tab_scales[0].bitcast(I32))
+        for r in range(4):
+            nc.sync.dma_start(w4_s_raw[r:P:32, :].bitcast(I32), w4_scales[0, r:16:4, :].bitcast(I32))
         nc.gpsimd.dma_start(gs_t[:], gs.rearrange("(b p t) -> p b t", b=2, t=4))
         tab_w = staged([P, T], U32, "tab_w", "slot3")
         nc.sync.dma_start(tab_w[:].bitcast(I32), tab_words[0].rearrange("p t i -> p (t i)").bitcast(I32))
-        load_scale_rows(nc.sync, w4_s_raw, w4_scales, range(4))
 
         def cast_views(raw_cols, name, tag="grouped", bufs=3):
             grouped = staged([P, 4 * N], BF16, name, tag, bufs=bufs)
@@ -102,23 +99,24 @@ def tile_list_brush_pressure_advice_kernel(
             )
 
         grouped, dst, src = cast_views(w1_raw0[:], "w1_g0", "slot1", 1)
-        nc.vector.tensor_scalar(dst, src, -1.0, None, op0=ALU.mult)
-        w1_q = [quantize(grouped, "w1_0")]
-        w8_raw = staged([P, 2, H], I32, "w8_raw", "slot0")
-        nc.sync.dma_start(w8_raw[:], w8_words.rearrange("a p c i -> p a (c i)").bitcast(I32))
+        nc.scalar.activation(dst, src, ACT.Copy, scale=-1.0)
 
-        gains = held([P, SLICES, N], F32, "gains")
-        gu_cols = gu_t[:].rearrange("p b t -> p (b t)")
-        for s in range(SLICES):
-            nc.scalar.activation(gains[:, s, :], gu_cols[:, s : s + 1].to_broadcast([P, N]), ACT.Copy)
-
-        v_s = held([P, S], U8, "v_s")
-        nc.vector.tensor_copy(v_s[:], tab_s[:].indirect(offs_t[:]))
+        v_s_rows = held([P, S], U8, "v_s_rows")
+        nc.vector.tensor_copy(v_s_rows[:], tab_s[:].indirect(offs_t[:]))
+        for q in range(4):
+            nc.sync.dma_start(
+                v_s[32 * q : 32 * q + 4, :].bitcast(I32), v_s_rows[4 * q : 4 * q + 4, :].bitcast(I32)
+            )
         nc.vector.tensor_copy(
             w4_s[:].rearrange("p (b t c i) -> p b c t i", b=2, t=4, i=16),
             w4_s_raw[:].rearrange("p (b c i t) -> p b c t i", b=2, t=4, i=16),
         )
-        v_w = [staged([P, N], U32, "v_w0", "slot2")[:], staged([P, N], U32, "v_w1", "planes")[:]]
+        w8_raw = staged([P, 2, H], I32, "w8_raw", "slot2")
+        nc.sync.dma_start(w8_raw[:], w8_words.rearrange("a p c i -> p a (c i)").bitcast(I32))
+        w1_q = [quantize(grouped, "w1_0")]
+        gains = staged([P, SLICES, N], F32, "gains", "slot1")
+        gu_cols = gu_t[:].rearrange("p b t -> p (b t)")
+        v_w = [held([P, N], U32, "v_w0")[:], held([P, N], U32, "v_w1")[:]]
         for u in range(2):
             nc.vector.tensor_copy(v_w[u], tab_w[:].indirect(offs_t[:, 32 * u : 32 * (u + 1)]))
         w8_c = held([P, 2, H], I32, "w8_c")
@@ -128,7 +126,7 @@ def tile_list_brush_pressure_advice_kernel(
                 w8_raw[:, a, :].rearrange("p (b c i t) -> p b c t i", b=2, t=4, i=4),
             )
 
-        w1_raw1 = load_rows(w1, 0, slice(N, H), "w1_raw1", "slot1")
+        w1_raw1 = load_rows(w1, 0, slice(N, H), "w1_raw1", "slot0")
         w2_raw = {}
         w2_raw0 = load_rows(w2, 0, slice(0, H), "w2_raw0", "slot3")
         w2_raw[0, 0] = w2_raw0[:, :, 0:N]
@@ -169,6 +167,7 @@ def tile_list_brush_pressure_advice_kernel(
                     stop=True,
                 )
                 nc.scalar.activation(silu[s][:, cols], acc[:], ACT.Silu)
+            nc.scalar.activation(gains[:, s, :], gu_cols[:, s : s + 1].to_broadcast([P, N]), ACT.Copy)
 
         def pick(s, first, second):
             t = s % 4
@@ -181,9 +180,9 @@ def tile_list_brush_pressure_advice_kernel(
         def larger(first, second, b):
             grouped = staged([P, 4 * N], BF16, f"x_g{b}", "grouped", bufs=3)
             nc.vector.tensor_tensor(
-                grouped[:].rearrange("p (c i t) -> p c t i", i=4, t=4),
-                first[:].rearrange("p t (c i) -> p c t i", i=4),
-                second[:].rearrange("p t (c i) -> p c t i", i=4),
+                grouped[:].rearrange("p (c i t) -> p c t i", i=2, t=4),
+                first[:].rearrange("p t (c i) -> p c t i", i=2),
+                second[:].rearrange("p t (c i) -> p c t i", i=2),
                 ALU.max,
             )
             return quantize(grouped, f"x_{b}")
@@ -199,14 +198,14 @@ def tile_list_brush_pressure_advice_kernel(
                 w8_s_raw[32 * q : 32 * q + 8, :].bitcast(I32), w8_scales[:, 4 * q : 4 * q + 4, :].bitcast(I32)
             )
         w1_q.append(quantize(cast_on_scalar(w1_raw1[:], "w1_g1", -1.0), "w1_1"))
-        w2_raw[1, 0] = load_rows(w2, 1, slice(0, N), "w2_raw10", "slot1")[:]
+        w2_raw[1, 0] = load_rows(w2, 1, slice(0, N), "w2_raw10", "slot0")[:]
         for s in range(4, SLICES):
             stage1(s)
 
         w8_s = held([P, H], U8, "w8_s")
         for b in range(2):
             if b == 0:
-                first = staged([P, 4, N], F32, f"first{b}", "slot0")
+                first = staged([P, 4, N], F32, f"first{b}", "slot2")
             else:
                 first = staged([P, 4, N], F32, f"first{b}", "picked", bufs=3)
             second = staged([P, 4, N], F32, f"second{b}", "picked", bufs=3)
@@ -214,7 +213,7 @@ def tile_list_brush_pressure_advice_kernel(
                 pick(4 * b + t, first, second)
             x_q.append(larger(first, second, b))
             if b == 0:
-                w2_raw[1, 1] = load_rows(w2, 1, slice(N, H), "w2_raw11", "slot0")[:]
+                w2_raw[1, 1] = load_rows(w2, 1, slice(N, H), "w2_raw11", "slot2")[:]
                 nc.vector.tensor_copy(
                     w8_s[:].rearrange("p (b t c i) -> p b c t i", b=2, t=4, i=16),
                     w8_s_raw[:].rearrange("p (b c i t) -> p b c t i", b=2, t=4, i=16),

import math
from contextlib import ExitStack

import concourse.mybir as mybir

K, H, T, S, NP = 512, 1024, 4096, 1024, 512
FLOPS = 2 * (2 * K * H * S) + 2 * (2 * H * H * NP)

F32 = mybir.dt.float32
BF16 = mybir.dt.bfloat16
I32 = mybir.dt.int32
U32 = mybir.dt.uint32
U16 = mybir.dt.uint16
U8 = mybir.dt.uint8
FP8X4 = mybir.dt.float8_e4m3fn_x4
FP4X4 = mybir.dt.float4_e2m1fn_x4
ALU = mybir.AluOpType
ACT = mybir.ActivationFunctionType

P = 128
N = 512
SLICES = H // P
TURN_OFFSET = float(2 ** 21)


def tile_list_brush_pressure_advice_kernel(
    tc, tab_words, tab_scales, offs, w1, w4_words, w4_scales, gu, pos1, pos2, w2, w8_words, w8_scales, pos3, gs, out
):
    nc = tc.nc
    with ExitStack() as ctx:
        lists = ctx.enter_context(tc.tile_pool(name="lists", bufs=1))
        keep = ctx.enter_context(tc.tile_pool(name="keep", bufs=1))
        ring = ctx.enter_context(tc.tile_pool(name="ring", bufs=1))
        psum = ctx.enter_context(tc.psum_pool(name="psum", bufs=8))

        def held(shape, dtype, name):
            return keep.tile(shape, dtype, name=name, align_bytes=64)

        def staged(shape, dtype, name, tag, bufs=1):
            return ring.tile(shape, dtype, name=name, tag=tag, bufs=bufs, align_bytes=64)

        warm_in = staged([P, 1], F32, "warm_in", "slot3")
        warm_out = held([P, 1], F32, "warm_out")
        tab_s = staged([P, T], U8, "tab_s", "slot2")
        nc.vector.memset(tab_s[:].bitcast(I32), 0)
        w4_s_raw = held([P, H], U8, "w4_s_raw")
        nc.vector.memset(w4_s_raw[:].bitcast(I32), 0)
        nc.vector.memset(warm_in[:], 0.0)
        nc.scalar.activation(warm_out[:], warm_in[:], ACT.Silu)
        v_s = held([P, S], U8, "v_s")
        nc.vector.memset(v_s[:].bitcast(I32), 0)

        offs_t = lists.tile([P, S // 16], U16, name="offs_t")
        pos1_t = lists.tile([P, NP // 16], U16, name="pos1_t")
        pos2_t = lists.tile([P, NP // 16], U16, name="pos2_t")
        pos3_t = lists.tile([P, S // 16], U16, name="pos3_t")
        for tile, src in ((offs_t, offs), (pos1_t, pos1), (pos2_t, pos2), (pos3_t, pos3)):
            nc.sync.dma_start(tile[:], src)

        gu_t = held([P, 2, 4], F32, "gu_t")
        gs_t = held([P, 2, 4], F32, "gs_t")
        nc.gpsimd.dma_start(gu_t[:], gu.rearrange("(b p t) -> p b t", b=2, t=4))

        def load_rows(w, a, cols, name, tag):
            raw = staged([P, 4, cols.stop - cols.start], F32, name, tag)
            nc.sync.dma_start(raw[:], w[N * a : N * (a + 1), cols].rearrange("(p j) c -> p j c", j=4))
            return raw

        w4_raw = held([P, 2 * H], U8, "w4_raw")
        nc.sync.dma_start(w4_raw[:].bitcast(I32), w4_words[0].bitcast(I32))

        w1_raw0 = load_rows(w1, 0, slice(0, N), "w1_raw0", "slot0")
        nc.sync.dma_start(tab_s[0:16, :].bitcast(I32), tab_scales[0].bitcast(I32))
        for r in range(4):
            nc.sync.dma_start(w4_s_raw[r:P:32, :].bitcast(I32), w4_scales[0, r:16:4, :].bitcast(I32))
        nc.gpsimd.dma_start(gs_t[:], gs.rearrange("(b p t) -> p b t", b=2, t=4))
        tab_w = staged([P, T], U32, "tab_w", "slot3")
        nc.sync.dma_start(tab_w[:].bitcast(I32), tab_words[0].rearrange("p t i -> p (t i)").bitcast(I32))

        def cast_views(raw_cols, name, tag="grouped", bufs=3):
            grouped = staged([P, 4 * N], BF16, name, tag, bufs=bufs)
            dst = grouped[:].rearrange("p (t m j) -> p m t j", t=4, j=4)
            src = raw_cols.rearrange("p j (m t) -> p m t j", t=4)
            return grouped, dst, src

        def quantize(grouped, name):
            codes = staged([P, N], U32, name + "_c", name + "_c")
            scales = held([P, N], U8, name + "_s")
            nc.vector.quantize_mx(out=codes[:].bitcast(FP8X4), scales=scales[:], in_=grouped[:])
            return codes, scales

        w4_c = held([P, 2 * H], U8, "w4_c")
        w4_s = held([P, H], U8, "w4_s")
        for b in range(2):
            cols = slice(H * b, H * (b + 1))
            nc.vector.tensor_copy(
                w4_c[:, cols].rearrange("p (t c i e) -> p c t i e", t=4, i=8, e=2),
                w4_raw[:, cols].rearrange("p (c i t e) -> p c t i e", t=4, i=8, e=2),
            )

        grouped, dst, src = cast_views(w1_raw0[:], "w1_g0", "slot1", 1)
        nc.scalar.activation(dst, src, ACT.Copy, scale=-1.0)

        v_s_rows = held([P, S], U8, "v_s_rows")
        nc.vector.tensor_copy(v_s_rows[:], tab_s[:].indirect(offs_t[:]))
        for q in range(4):
            nc.sync.dma_start(
                v_s[32 * q : 32 * q + 4, :].bitcast(I32), v_s_rows[4 * q : 4 * q + 4, :].bitcast(I32)
            )
        nc.vector.tensor_copy(
            w4_s[:].rearrange("p (b t c i) -> p b c t i", b=2, t=4, i=16),
            w4_s_raw[:].rearrange("p (b c i t) -> p b c t i", b=2, t=4, i=16),
        )
        w8_raw = staged([P, 2, H], I32, "w8_raw", "slot2")
        nc.sync.dma_start(w8_raw[:], w8_words.rearrange("a p c i -> p a (c i)").bitcast(I32))
        w1_q = [quantize(grouped, "w1_0")]
        gains = staged([P, SLICES, N], F32, "gains", "slot1")
        gu_cols = gu_t[:].rearrange("p b t -> p (b t)")
        v_w = [held([P, N], U32, "v_w0")[:], held([P, N], U32, "v_w1")[:]]
        for u in range(2):
            nc.vector.tensor_copy(v_w[u], tab_w[:].indirect(offs_t[:, 32 * u : 32 * (u + 1)]))
        w8_c = held([P, 2, H], I32, "w8_c")
        for a in range(2):
            nc.vector.tensor_copy(
                w8_c[:, a, :].rearrange("p (b t c i) -> p b c t i", b=2, t=4, i=4),
                w8_raw[:, a, :].rearrange("p (b c i t) -> p b c t i", b=2, t=4, i=4),
            )

        w1_raw1 = load_rows(w1, 0, slice(N, H), "w1_raw1", "slot0")
        w2_raw = {}
        w2_raw0 = load_rows(w2, 0, slice(0, H), "w2_raw0", "slot3")
        w2_raw[0, 0] = w2_raw0[:, :, 0:N]
        w2_raw[0, 1] = w2_raw0[:, :, N:H]

        gg = held([P, SLICES], F32, "gg")
        nc.gpsimd.tensor_tensor(gg[:], gu_cols, gs_t[:].rearrange("p b t -> p (b t)"), ALU.mult)

        def cast_on_scalar(raw_cols, name, scale):
            grouped, dst, src = cast_views(raw_cols, name)
            nc.scalar.activation(dst, src, ACT.Copy, scale=scale)
            return grouped

        silu = [held([P, S], F32, f"silu{s}") for s in range(SLICES)]

        def stage1(s):
            b, t = divmod(s, 4)
            w1_c, w1_s = w1_q[b]
            for u in range(2):
                cols = slice(N * u, N * (u + 1))
                acc = psum.tile([P, N], F32, name="acc", tag="bank")
                nc.tensor.matmul_mx(
                    out=acc[:],
                    lhsT=w4_c[:, 2 * P * s : 2 * P * (s + 1)].bitcast(FP4X4),
                    lhsT_scale=w4_s[:, P * s : P * (s + 1)],
                    rhs=v_w[u].bitcast(FP8X4),
                    rhs_scale=v_s[:, cols],
                    start=True,
                    stop=False,
                )
                nc.tensor.matmul_mx(
                    out=acc[:],
                    lhsT=w1_c[:, P * t : P * (t + 1)].bitcast(FP8X4),
                    lhsT_scale=w1_s[:, P * t : P * (t + 1)],
                    rhs=v_w[u].bitcast(FP8X4),
                    rhs_scale=v_s[:, cols],
                    start=False,
                    stop=True,
                )
                nc.scalar.activation(silu[s][:, cols], acc[:], ACT.Silu)
            nc.scalar.activation(gains[:, s, :], gu_cols[:, s : s + 1].to_broadcast([P, N]), ACT.Copy)

        def pick(s, first, second):
            t = s % 4
            nc.vector.tensor_tensor(first[:, t, :], silu[s][:].indirect(pos1_t[:]), gains[:, s, :], ALU.mult)
            nc.vector.tensor_tensor(second[:, t, :], silu[s][:].indirect(pos2_t[:]), gains[:, s, :], ALU.mult)

        def own_part(s):
            nc.scalar.activation(silu[s][:], silu[s][:], ACT.Copy, scale=gg[:, s : s + 1], bias=-1.0)

        def larger(first, second, b):
            grouped = staged([P, 4 * N], BF16, f"x_g{b}", "grouped", bufs=3)
            nc.vector.tensor_tensor(
                grouped[:].rearrange("p (c i t) -> p c t i", i=2, t=4),
                first[:].rearrange("p t (c i) -> p c t i", i=2),
                second[:].rearrange("p t (c i) -> p c t i", i=2),
                ALU.max,
            )
            return quantize(grouped, f"x_{b}")

        x_q = []
        w2_q = {}
        for s in range(4):
            stage1(s)
        w8_s_raw = staged([P, H], U8, "w8_s_raw", "w1_0_c")
        nc.vector.memset(w8_s_raw[:].bitcast(I32), 0)
        for q in range(4):
            nc.sync.dma_start(
                w8_s_raw[32 * q : 32 * q + 8, :].bitcast(I32), w8_scales[:, 4 * q : 4 * q + 4, :].bitcast(I32)
            )
        w1_q.append(quantize(cast_on_scalar(w1_raw1[:], "w1_g1", -1.0), "w1_1"))
        w2_raw[1, 0] = load_rows(w2, 1, slice(0, N), "w2_raw10", "slot0")[:]
        for s in range(4, SLICES):
            stage1(s)

        w8_s = held([P, H], U8, "w8_s")
        for b in range(2):
            if b == 0:
                first = staged([P, 4, N], F32, f"first{b}", "slot2")
            else:
                first = staged([P, 4, N], F32, f"first{b}", "picked", bufs=3)
            second = staged([P, 4, N], F32, f"second{b}", "picked", bufs=3)
            for t in range(4):
                pick(4 * b + t, first, second)
            x_q.append(larger(first, second, b))
            if b == 0:
                w2_raw[1, 1] = load_rows(w2, 1, slice(N, H), "w2_raw11", "slot2")[:]
                nc.vector.tensor_copy(
                    w8_s[:].rearrange("p (b t c i) -> p b c t i", b=2, t=4, i=16),
                    w8_s_raw[:].rearrange("p (b c i t) -> p b c t i", b=2, t=4, i=16),
                )
                for c in range(2):
                    for a in range(2):
                        w2_q[a, c] = quantize(cast_on_scalar(w2_raw[a, c], f"w2_g{a}{c}", 1.0), f"w2_{a}{c}")
                for s in range(4):
                    own_part(s)

        out_rows = out.rearrange("(b p t) j -> b t p j", b=2, t=4)
        work = {}

        def products(s):
            b, t = divmod(s, 4)
            m_cols = slice(P * t, P * (t + 1))
            n_cols = slice(P * s, P * (s + 1))
            acc2 = psum.tile([P, N], F32, name="acc2", tag="bank")
            acc8 = psum.tile([P, N], F32, name="acc8", tag="bank")
            for a in range(2):
                nc.tensor.matmul_mx(
                    out=acc8[:],
                    lhsT=w8_c[:, a, n_cols].bitcast(FP8X4),
                    lhsT_scale=w8_s[4 * a :, n_cols],
                    rhs=x_q[a][0][:].bitcast(FP8X4),
                    rhs_scale=x_q[a][1][:],
                    start=(a == 0),
                    stop=(a == 1),
                )
            for a in range(2):
                nc.tensor.matmul_mx(
                    out=acc2[:],
                    lhsT=w2_q[a, b][0][:, m_cols].bitcast(FP8X4),
                    lhsT_scale=w2_q[a, b][1][:, m_cols],
                    rhs=x_q[a][0][:].bitcast(FP8X4),
                    rhs_scale=x_q[a][1][:],
                    start=(a == 0),
                    stop=(a == 1),
                )
            work[s] = staged([P, 3 * N], F32, f"work{s}", "work", bufs=4)
            w_b, w_c = work[s][:, N : 2 * N], work[s][:, 2 * N : 3 * N]
            nc.scalar.activation(w_b, acc8[:], ACT.Copy, scale=1.0 / (2.0 * math.pi))
            nc.vector.scalar_tensor_tensor(w_c, acc2[:], 1.0 / (2.0 * math.pi), w_b, ALU.mult, ALU.max)

        def reduce_turns(s):
            w_a, w_c = work[s][:, 0:N], work[s][:, 2 * N : 3 * N]
            whole = staged([P, N], U32, f"whole{s}", "whole", bufs=3)
            nc.scalar.activation(whole[:], w_c, ACT.Copy, bias=TURN_OFFSET + 0.75)
            nc.vector.scalar_tensor_tensor(
                w_a, whole[:].bitcast(I32), TURN_OFFSET + 0.5, w_c, ALU.subtract, ALU.subtract
            )

        def finish(s):
            b, t = divmod(s, 4)
            w_a, w_b = work[s][:, 0:N], work[s][:, N : 2 * N]
            nc.scalar.activation(w_b, w_a, ACT.Sin, scale=math.pi)
            nc.scalar.activation(w_a, w_b, ACT.Square, scale=math.sqrt(2.0))
            result = staged([P, S], F32, f"result{s}", "picked", bufs=3)
            if s < SLICES - 1:
                nc.vector.tensor_tensor(result[:], work[s][:].indirect(pos3_t[:]), silu[s][:], ALU.add)
                nc.sync.dma_start(out_rows[b, t], result[:])
            else:
                for lo, hi in ((0, 512), (512, 768), (768, 1024)):
                    cols = slice(lo, hi)
                    nc.vector.tensor_tensor(
                        result[:, cols], work[s][:].indirect(pos3_t[:, lo // 16 : hi // 16]), silu[s][:, cols], ALU.add
                    )
                    nc.sync.dma_start(out_rows[b, t][:, cols], result[:, cols])

        for step in range(SLICES + 2):
            if step < SLICES:
                products(step)
            if 1 <= step <= SLICES:
                reduce_turns(step - 1)
            if step >= 2:
                finish(step - 2)
                if step + 2 < SLICES:
                    own_part(step + 2)
